import numpy as np
CORES = [0,1,2,3,4,5,6,7,8,9,10,11,12,13,14,15,16,17,18,19,20,21,22,23,24,25,26,27,28,29,30,31,32,33,34,35,36,37,38,39,40,41,42,43,44,45,46,47,48,49,50,51,52,53,54,55,56,57,58,59,60,61,62,63,64,65,66,67,68,69,70,71,72,73,74,75,76,77,78,79,80,81,82,83,84,85,86,87,88,89,90,91,92,93,94,95,96,97,98,99,100,101,102,103,104,105,106,107,108,109,110,111,112,113,114,115,116,117,118,119,120,121,122,123,124,125,126,127,128,129,130,131,132,133,134,135,136,137,138,139,140,141,142,143,144,145,146,147,148,149,150,151,152,153,154,155,156,157,158,159,160,161,162,163,164,165,166,167,168,169,170,171,172,173,174,175,176,177,178,179,180,181,182,183,184,185,186,187,188,189,190,191,192,193,194,195,196,197,198,199,200,201,202,203,204,205,206,207,208,209,210,211,212,213,214,215,216,217,218,219,220,221,222,223,224,225,226,227,228,229,230,231,232,233,234,235,236,237,238,239,240,241,242,243,244,245,246,247,248,249,250,251,252,253,254,255,256,257,258,259,260,261,262,263,264,265,266,267,268,269,270,271,272,273,274,275,276,277,278,279,280,281,282,283,284,285,286,287,288,289,290,291,292,293,294,295,296,297,298,299,300,301,302,303,304,305,306,307,308,309,310,311,312,313,314,315,316,317,318,319,320,321,322,323,324,325,326,327,328,329,330,331,332,333,334,335,336,337,338,339,340,341,342,343,344,345,346,347,348,349,350,351,352,353,354,355,356,357,358,359,360,361,362,363,364,365,366,367,368,369,370,371,372,373,374,375,376,377,378,379,380,381,382,383,384,385,386,387,388,389,390,391,392,393,394,395,396,397,398,399,400,401,402,403,404,405,406,407,408,409,410,411,412,413,414,415,416,417,418,419,420,421,422,423,424,425,426,427,428,429,430,431,432,433,434,435,436,437,438,439,440,441,442,443,444,445,446,447,448,449,450,451,452,453,454,455,456,457,458,459,460,461,462,463,464,465,466,467,468,469,470,471,472,473,474,475,476,477,478,479,480,481,482,483,484,485,486,487,488,489,490,491,492,493,494,495,496,497,498,499,500,501,502,503,504,505,506,507,508,509,510,511]
N = 512
GROUPS = [[h * 128 + (m * j + a) % 128 for h, (m, a) in enumerate(((1, 0), (5, 3), (13, 40), (29, 77)))] for j in range(128)]
def setup_inputs(rng):
    return {"x": rng.standard_normal((N, 128, 128)).astype(np.float32)}
def reference(x):
    y = np.empty((N, 128, 4 * 128), x.dtype)
    for g in GROUPS:
        cat = np.concatenate([x[r] for r in g], axis=1)
        for r in g:
            y[r] = cat
    return {"y": y}

@@ -1,0 +1,108 @@
+import concourse.bass as bass
+
+W = 128
+SLOTS = 6
+LEVELS = 4
+SCRATCH = {
+    "land": ("sbuf", [128, 4 * W], "float32"),
+    "hold": ("sbuf", [128, SLOTS * W], "float32"),
+}
+SEMAPHORES = ["loaded", "got1", "got2", "got3", "got4", "sent", "stored"]
+
+CACHE = {}
+
+
+def build(T, topo):
+    groups = T.tables["GROUPS"]
+    writes = []
+
+    def send(level, src, blk, tree):
+        far = []
+        for dst, sub in tree:
+            if topo.may_write(src, dst):
+                writes.append((level, src, blk, dst))
+                send(level + 1, dst, blk, sub)
+            else:
+                far.append((dst, sub))
+        if far:
+            r = (src & ~3) | 2 | (src & 1)
+            writes.append((level, src, blk, r))
+            send(level + 1, r, blk, far)
+
+    part = [1, 0, 3, 2]
+    cross = [3, 2, 1, 0]
+    for grp in groups:
+        for s in range(4):
+            c = cross[s]
+            send(1, grp[s], grp[s], [(grp[part[s]], []), (grp[c], [(grp[part[c]], [])])])
+    return finish(groups, writes)
+
+
+def finish(groups, writes):
+    where = {}
+    for grp in groups:
+        for c in grp:
+            for k, b in enumerate(grp):
+                where[(c, b)] = ("land", k)
+    used = {}
+    for level, src, blk, dst in writes:
+        if (dst, blk) not in where:
+            n = used.get(dst, 0)
+            used[dst] = n + 1
+            where[(dst, blk)] = ("hold", n)
+    calls = {}
+    for level, src, blk, dst in writes:
+        calls.setdefault((src, level), {}).setdefault(blk, []).append(dst)
+    expect = {}
+    sent = {}
+    prog = {}
+    for (src, level), per in calls.items():
+        m = len(per)
+        n = 8
+        while n * m > 8:
+            n //= 2
+        items = []
+        for i, blk in enumerate(sorted(per)):
+            mask = ((1 << n) - 1) << (i * n)
+            items.append((blk, per[blk], mask))
+            sent[src] = sent.get(src, 0) + n
+            for d in per[blk]:
+                expect[(d, level)] = expect.get((d, level), 0) + n
+        prog[(src, level)] = items
+    return {"where": where, "prog": prog, "expect": expect, "sent": sent}
+
+
+def rank_program(g, core, T, topo):
+    if "plan" not in CACHE:
+        CACHE["plan"] = build(T, topo)
+    plan = CACHE["plan"]
+    where = plan["where"]
+    bufs = {"land": T.land, "hold": T.hold}
+    got = [T.sem.got1, T.sem.got2, T.sem.got3, T.sem.got4]
+
+    def ap(c, blk):
+        name, k = where[(c, blk)]
+        return bufs[name][:, k * W:(k + 1) * W]
+
+    g.dma_start(out=ap(core, core), in_=T.x[:, :]).then_inc(T.sem.loaded, 16)
+    g.wait_ge(T.sem.loaded, 16)
+    for level in range(1, LEVELS + 1):
+        items = plan["prog"].get((core, level))
+        if items:
+            trs = []
+            for blk, dsts, mask in items:
+                ids = []
+                for d in dsts:
+                    rid, pid = topo.addr(d, core)
+                    ids.append(bass.DstId(rid=rid, pnc=pid))
+                trs.append(bass.RemoteDMATransfer(dst_ids=ids, dma_engine_mask=mask, remote_sem=got[level - 1],
+                                                  srcs=[ap(core, blk)], dsts=[ap(d, blk) for d in dsts]))
+            g.remote_dma_fused(trs, local_sem=T.sem.sent)
+        n = plan["expect"].get((core, level), 0)
+        if n:
+            g.wait_ge(got[level - 1], n)
+    n = plan["sent"].get(core, 0)
+    if n:
+        g.wait_ge(T.sem.sent, n)
+    g.dma_start(out=T.y[:, :], in_=T.land[:, :]).then_inc(T.sem.stored, 16)
+    g.wait_ge(T.sem.stored, 16)

@@ -1,74 +1,92 @@
 import concourse.bass as bass
 
 W = 128
-SLOTS = 6
-LEVELS = 4
+HOLD = 2
 SCRATCH = {
     "land": ("sbuf", [128, 4 * W], "float32"),
-    "hold": ("sbuf", [128, SLOTS * W], "float32"),
+    "hold": ("sbuf", [128, HOLD * W], "float32"),
 }
-SEMAPHORES = ["loaded", "got1", "got2", "got3", "got4", "sent", "stored"]
+SEMAPHORES = ["loaded", "near1", "far1", "got2", "got3", "sent", "stored"]
+
+TABLE = """10013 10003 20330 33035 33020;11300 11320 22035;12035 12023 22313 31300;13520 13537 23700 30013
+10102 20210 20232 33225;11017 21701 21727 32725 32732;12527 22732 22712 31210 31201;13225 13207 20701 20710
+10215 10201 20137 33722;11516 21602 21622 32237;12237 12215 21516 31602;13722 13731 23102 30215
+10312 10300 20033 33334 33327;11203 11227 22734;12734 23403 30312;13437 13403 23727 20312
+10417 10431 23132 33224;11704 20433 33331 33324;12426 22631 22617 31704;13136 13104 23624 20417
+10506 20614 20636 33621;11412 11421 21205 22136;12136 12114 21417 31705;13621 22113 31314 31305
+10611 21126 32633;11106 11126 22633;12633 12624 22411 31106;13326 13306 20611
+10716 10730 23032 33223;11607 11615 21523 32330;12330 12325 22516 31607;13036 23623 23607 30716"""
 
 CACHE = {}
 
 
 def build(T, topo):
     groups = T.tables["GROUPS"]
+    table = [[[tuple(int(ch) for ch in tok) for tok in blk.split()] for blk in line.split(";")]
+             for line in TABLE.split("\n")]
     writes = []
-
-    def send(level, src, blk, tree):
-        far = []
-        for dst, sub in tree:
-            if topo.may_write(src, dst):
-                writes.append((level, src, blk, dst))
-                send(level + 1, dst, blk, sub)
-            else:
-                far.append((dst, sub))
-        if far:
-            r = (src & ~3) | 2 | (src & 1)
-            writes.append((level, src, blk, r))
-            send(level + 1, r, blk, far)
-
-    part = [1, 0, 3, 2]
-    cross = [3, 2, 1, 0]
-    for grp in groups:
+    for j, grp in enumerate(groups):
+        base = [c - c % 8 for c in grp]
         for s in range(4):
-            c = cross[s]
-            send(1, grp[s], grp[s], [(grp[part[s]], []), (grp[c], [(grp[part[c]], [])])])
-    return finish(groups, writes)
-
-
-def finish(groups, writes):
+            ws = table[j % 8][s]
+            came = {}
+            feeds = set((hs, i) for lev, hs, i, hd, k in ws)
+            for lev, hs, i, hd, k in sorted(ws):
+                src = base[hs] + i
+                dst = base[hd] + k
+                crosses = (hs // 2) != (hd // 2)
+                if not topo.may_write(src, dst) or src == dst:
+                    raise ValueError("write %d -> %d is not allowed" % (src, dst))
+                if lev == 1 and src != grp[s]:
+                    raise ValueError("level 1 write not from the owner")
+                if lev > 1 and src not in came:
+                    raise ValueError("core %d sends a block it has not got" % src)
+                writes.append([lev, src, grp[s], dst, crosses, came.get(src, False), (hd, k) not in feeds])
+                came[dst] = crosses
+            for c in grp:
+                if c != grp[s] and c not in came:
+                    raise ValueError("block not delivered")
+    slots = {}
+    for w in writes:
+        slot = 0 if w[0] == 1 else (3 if w[0] == 3 else (2 if w[5] else 1))
+        slots.setdefault(w[1], {}).setdefault(slot, []).append(w)
+    for src, per in slots.items():
+        if 1 in per and 2 in per and 3 in per and all(w[6] for w in per[2]):
+            per[3] = per[3] + per.pop(2)
+        if 1 in per and 2 in per and all(w[6] and not w[4] for w in per[1]):
+            per[2] = per[2] + per.pop(1)
     where = {}
     for grp in groups:
         for c in grp:
             for k, b in enumerate(grp):
                 where[(c, b)] = ("land", k)
     used = {}
-    for level, src, blk, dst in writes:
-        if (dst, blk) not in where:
-            n = used.get(dst, 0)
-            used[dst] = n + 1
-            where[(dst, blk)] = ("hold", n)
-    calls = {}
-    for level, src, blk, dst in writes:
-        calls.setdefault((src, level), {}).setdefault(blk, []).append(dst)
+    for w in writes:
+        if (w[3], w[2]) not in where:
+            n = used.get(w[3], 0)
+            if n >= HOLD:
+                raise ValueError("too many held blocks")
+            used[w[3]] = n + 1
+            where[(w[3], w[2])] = ("hold", n)
+    prog = {}
     expect = {}
     sent = {}
-    prog = {}
-    for (src, level), per in calls.items():
-        m = len(per)
-        n = 8
-        while n * m > 8:
-            n //= 2
-        items = []
-        for i, blk in enumerate(sorted(per)):
-            mask = ((1 << n) - 1) << (i * n)
-            items.append((blk, per[blk], mask))
-            sent[src] = sent.get(src, 0) + n
-            for d in per[blk]:
-                expect[(d, level)] = expect.get((d, level), 0) + n
-        prog[(src, level)] = items
+    for src, per in slots.items():
+        for slot, ws in per.items():
+            trs = {}
+            for w in ws:
+                sem = (1 if w[4] else 0) if slot == 0 else (2 if slot < 3 else 3)
+                trs.setdefault((w[2], sem), []).append(w[3])
+            n = 8
+            while n * len(trs) > 8:
+                n //= 2
+            items = []
+            for q, key in enumerate(sorted(trs)):
+                items.append((key[0], key[1], trs[key], ((1 << n) - 1) << (q * n)))
+                sent[src] = sent.get(src, 0) + n
+                for d in trs[key]:
+                    expect[(d, key[1])] = expect.get((d, key[1]), 0) + n
+            prog[(src, slot)] = items
     return {"where": where, "prog": prog, "expect": expect, "sent": sent}
 
 
@@ -78,29 +96,41 @@ def rank_program(g, core, T, topo):
     plan = CACHE["plan"]
     where = plan["where"]
     bufs = {"land": T.land, "hold": T.hold}
-    got = [T.sem.got1, T.sem.got2, T.sem.got3, T.sem.got4]
+    sems = [T.sem.near1, T.sem.far1, T.sem.got2, T.sem.got3]
 
     def ap(c, blk):
         name, k = where[(c, blk)]
         return bufs[name][:, k * W:(k + 1) * W]
 
+    def call(slot):
+        items = plan["prog"].get((core, slot))
+        if not items:
+            return
+        trs = []
+        for blk, sem, dsts, mask in items:
+            ids = []
+            for d in dsts:
+                rid, pid = topo.addr(d, core)
+                ids.append(bass.DstId(rid=rid, pnc=pid))
+            trs.append(bass.RemoteDMATransfer(dst_ids=ids, dma_engine_mask=mask, remote_sem=sems[sem],
+                                              srcs=[ap(core, blk)], dsts=[ap(d, blk) for d in dsts]))
+        g.remote_dma_fused(trs, local_sem=T.sem.sent)
+
+    def wait(sem):
+        n = plan["expect"].get((core, sem), 0)
+        if n:
+            g.wait_ge(sems[sem], n)
+
     g.dma_start(out=ap(core, core), in_=T.x[:, :]).then_inc(T.sem.loaded, 16)
     g.wait_ge(T.sem.loaded, 16)
-    for level in range(1, LEVELS + 1):
-        items = plan["prog"].get((core, level))
-        if items:
-            trs = []
-            for blk, dsts, mask in items:
-                ids = []
-                for d in dsts:
-                    rid, pid = topo.addr(d, core)
-                    ids.append(bass.DstId(rid=rid, pnc=pid))
-                trs.append(bass.RemoteDMATransfer(dst_ids=ids, dma_engine_mask=mask, remote_sem=got[level - 1],
-                                                  srcs=[ap(core, blk)], dsts=[ap(d, blk) for d in dsts]))
-            g.remote_dma_fused(trs, local_sem=T.sem.sent)
-        n = plan["expect"].get((core, level), 0)
-        if n:
-            g.wait_ge(got[level - 1], n)
+    call(0)
+    wait(0)
+    call(1)
+    wait(1)
+    call(2)
+    wait(2)
+    call(3)
+    wait(3)
     n = plan["sent"].get(core, 0)
     if n:
         g.wait_ge(T.sem.sent, n)

@@ -8,14 +8,14 @@ SCRATCH = {
 }
 SEMAPHORES = ["loaded", "near1", "far1", "got2", "got3", "sent", "stored"]
 
-TABLE = """10013 10003 20330 33035 33020;11300 11320 22035;12035 12023 22313 31300;13520 13537 23700 30013
-10102 20210 20232 33225;11017 21701 21727 32725 32732;12527 22732 22712 31210 31201;13225 13207 20701 20710
-10215 10201 20137 33722;11516 21602 21622 32237;12237 12215 21516 31602;13722 13731 23102 30215
-10312 10300 20033 33334 33327;11203 11227 22734;12734 23403 30312;13437 13403 23727 20312
-10417 10431 23132 33224;11704 20433 33331 33324;12426 22631 22617 31704;13136 13104 23624 20417
-10506 20614 20636 33621;11412 11421 21205 22136;12136 12114 21417 31705;13621 22113 31314 31305
-10611 21126 32633;11106 11126 22633;12633 12624 22411 31106;13326 13306 20611
-10716 10730 23032 33223;11607 11615 21523 32330;12330 12325 22516 31607;13036 23623 23607 30716"""
+TABLE = """10003 10013 20335 33520;11300 11320 22035;12023 22310 22335 31000 31013;13520 13536 23600 30013
+10102 20210 20232 33225;11017 21701 21722 32225 32232;12527 22712 22732 31201 31210;13201 13225 20103 30310
+10200 10215 20034 33422 33437;11516 21602 21624 32422 32437;12215 12237 21516 31602;13730 23002 23022 30215
+10301 10312 20133 33327 33334;11203 11225 22527 32734;12734 23405 30503 30512;13403 13437 20312 23727
+10417 10431 23132 33224;11704 20436 33624 33631;12426 22617 22631 31704;13104 13133 20417 23324
+10507 20714 20736 33621;11413 11421 21305 22136;12114 12136 21417 31705;13621 22113 31305 31314
+10611 21126 32633;11106 11126 22633;12633 23306 30611;13324 22411 22426 31106
+10716 10730 23032 33223;11615 21507 21523 32330;12325 12330 22516 31607;13037 23707 23723 30716"""
 
 CACHE = {}
 

@@ -8,15 +8,16 @@ SCRATCH = {
 }
 SEMAPHORES = ["loaded", "near1", "far1", "got2", "got3", "sent", "stored"]
 
-TABLE = """10003 10013 20335 33520;11300 11320 22035;12023 22310 22335 31000 31013;13520 13536 23600 30013
+TABLE = """10003 10013 20335 33520;11300 11320 22035;12022 12035 22213 31300;13520 13536 23600 30013
 10102 20210 20232 33225;11017 21701 21722 32225 32232;12527 22712 22732 31201 31210;13201 13225 20103 30310
-10200 10215 20034 33422 33437;11516 21602 21624 32422 32437;12215 12237 21516 31602;13730 23002 23022 30215
-10301 10312 20133 33327 33334;11203 11225 22527 32734;12734 23405 30503 30512;13403 13437 20312 23727
+10200 10215 20037 33722;11516 21602 21624 32422 32437;12215 12237 21516 31602;13731 23102 23122 30215
+10301 20112 20133 33327 33334;11203 11227 22734;12734 23405 30503 30512;13403 13437 20312 23727
 10417 10431 23132 33224;11704 20436 33624 33631;12426 22617 22631 31704;13104 13133 20417 23324
-10507 20714 20736 33621;11413 11421 21305 22136;12114 12136 21417 31705;13621 22113 31305 31314
+10507 20714 20736 33621;11412 11421 21205 22136;12114 12136 21417 31705;13621 22113 31305 31314
 10611 21126 32633;11106 11126 22633;12633 23306 30611;13324 22411 22426 31106
 10716 10730 23032 33223;11615 21507 21523 32330;12325 12330 22516 31607;13037 23707 23723 30716"""
 
+NEAR1, FAR1, GOT2, GOT3 = 0, 1, 2, 3
 CACHE = {}
 
 
@@ -26,113 +27,110 @@ def build(T, topo):
              for line in TABLE.split("\n")]
     writes = []
     for j, grp in enumerate(groups):
-        base = [c - c % 8 for c in grp]
+        chip = [c - c % 8 for c in grp]
         for s in range(4):
-            ws = table[j % 8][s]
+            route = table[j % 8][s]
+            senders = set((a, i) for lev, a, i, b, k in route)
             came = {}
-            feeds = set((hs, i) for lev, hs, i, hd, k in ws)
-            for lev, hs, i, hd, k in sorted(ws):
-                src = base[hs] + i
-                dst = base[hd] + k
-                crosses = (hs // 2) != (hd // 2)
-                if not topo.may_write(src, dst) or src == dst:
-                    raise ValueError("write %d -> %d is not allowed" % (src, dst))
-                if lev == 1 and src != grp[s]:
-                    raise ValueError("level 1 write not from the owner")
-                if lev > 1 and src not in came:
-                    raise ValueError("core %d sends a block it has not got" % src)
-                writes.append([lev, src, grp[s], dst, crosses, came.get(src, False), (hd, k) not in feeds])
+            for lev, a, i, b, k in sorted(route):
+                src, dst = chip[a] + i, chip[b] + k
+                if not topo.may_write(src, dst):
+                    raise ValueError("core %d may not write to core %d" % (src, dst))
+                if (src != grp[s]) if lev == 1 else (src not in came):
+                    raise ValueError("core %d does not hold the block it sends" % src)
+                crosses = topo.rack(a) != topo.rack(b)
+                writes.append([lev, src, grp[s], dst, crosses, came.get(src, False), (b, k) not in senders])
                 came[dst] = crosses
-            for c in grp:
-                if c != grp[s] and c not in came:
-                    raise ValueError("block not delivered")
-    slots = {}
+            if any(c != grp[s] and c not in came for c in grp):
+                raise ValueError("a member is left without a block")
+
+    stages = {}
     for w in writes:
-        slot = 0 if w[0] == 1 else (3 if w[0] == 3 else (2 if w[5] else 1))
-        slots.setdefault(w[1], {}).setdefault(slot, []).append(w)
-    for src, per in slots.items():
+        stage = 0 if w[0] == 1 else (3 if w[0] == 3 else (2 if w[5] else 1))
+        stages.setdefault(w[1], {}).setdefault(stage, []).append(w)
+    for per in stages.values():
         if 1 in per and 2 in per and 3 in per and all(w[6] for w in per[2]):
             per[3] = per[3] + per.pop(2)
         if 1 in per and 2 in per and all(w[6] and not w[4] for w in per[1]):
             per[2] = per[2] + per.pop(1)
+
     where = {}
     for grp in groups:
         for c in grp:
             for k, b in enumerate(grp):
                 where[(c, b)] = ("land", k)
-    used = {}
+    held = {}
     for w in writes:
         if (w[3], w[2]) not in where:
-            n = used.get(w[3], 0)
+            n = held.get(w[3], 0)
             if n >= HOLD:
-                raise ValueError("too many held blocks")
-            used[w[3]] = n + 1
+                raise ValueError("core %d holds too many blocks" % w[3])
+            held[w[3]] = n + 1
             where[(w[3], w[2])] = ("hold", n)
-    prog = {}
-    expect = {}
-    sent = {}
-    for src, per in slots.items():
-        for slot, ws in per.items():
-            trs = {}
+
+    calls, due, sent = {}, {}, {}
+    for src, per in stages.items():
+        for stage, ws in per.items():
+            transfers = {}
             for w in ws:
-                sem = (1 if w[4] else 0) if slot == 0 else (2 if slot < 3 else 3)
-                trs.setdefault((w[2], sem), []).append(w[3])
+                if stage == 0:
+                    sem = FAR1 if (w[4] and 1 in stages.get(w[3], {})) else NEAR1
+                else:
+                    sem = GOT2 if stage < 3 else GOT3
+                transfers.setdefault((w[2], sem), []).append(w[3])
             n = 8
-            while n * len(trs) > 8:
+            while n * len(transfers) > 8:
                 n //= 2
             items = []
-            for q, key in enumerate(sorted(trs)):
-                items.append((key[0], key[1], trs[key], ((1 << n) - 1) << (q * n)))
+            for q, key in enumerate(sorted(transfers)):
+                items.append((key[0], key[1], transfers[key], ((1 << n) - 1) << (q * n)))
                 sent[src] = sent.get(src, 0) + n
-                for d in trs[key]:
-                    expect[(d, key[1])] = expect.get((d, key[1]), 0) + n
-            prog[(src, slot)] = items
-    return {"where": where, "prog": prog, "expect": expect, "sent": sent}
+                for d in transfers[key]:
+                    due[(d, key[1])] = due.get((d, key[1]), 0) + n
+            calls[(src, stage)] = items
+    return {"where": where, "calls": calls, "due": due, "sent": sent}
 
 
 def rank_program(g, core, T, topo):
     if "plan" not in CACHE:
         CACHE["plan"] = build(T, topo)
     plan = CACHE["plan"]
-    where = plan["where"]
     bufs = {"land": T.land, "hold": T.hold}
     sems = [T.sem.near1, T.sem.far1, T.sem.got2, T.sem.got3]
 
-    def ap(c, blk):
-        name, k = where[(c, blk)]
+    def at(c, blk):
+        name, k = plan["where"][(c, blk)]
         return bufs[name][:, k * W:(k + 1) * W]
 
-    def call(slot):
-        items = plan["prog"].get((core, slot))
+    def call(stage):
+        items = plan["calls"].get((core, stage))
         if not items:
             return
-        trs = []
+        transfers = []
         for blk, sem, dsts, mask in items:
             ids = []
             for d in dsts:
                 rid, pid = topo.addr(d, core)
                 ids.append(bass.DstId(rid=rid, pnc=pid))
-            trs.append(bass.RemoteDMATransfer(dst_ids=ids, dma_engine_mask=mask, remote_sem=sems[sem],
-                                              srcs=[ap(core, blk)], dsts=[ap(d, blk) for d in dsts]))
-        g.remote_dma_fused(trs, local_sem=T.sem.sent)
+            transfers.append(bass.RemoteDMATransfer(dst_ids=ids, dma_engine_mask=mask, remote_sem=sems[sem],
+                                                    srcs=[at(core, blk)], dsts=[at(d, blk) for d in dsts]))
+        g.remote_dma_fused(transfers, local_sem=T.sem.sent)
 
     def wait(sem):
-        n = plan["expect"].get((core, sem), 0)
+        n = plan["due"].get((core, sem), 0)
         if n:
             g.wait_ge(sems[sem], n)
 
-    g.dma_start(out=ap(core, core), in_=T.x[:, :]).then_inc(T.sem.loaded, 16)
+    g.dma_start(out=at(core, core), in_=T.x[:, :]).then_inc(T.sem.loaded, 16)
     g.wait_ge(T.sem.loaded, 16)
     call(0)
-    wait(0)
+    wait(NEAR1)
     call(1)
-    wait(1)
+    wait(FAR1)
     call(2)
-    wait(2)
+    wait(GOT2)
     call(3)
-    wait(3)
-    n = plan["sent"].get(core, 0)
-    if n:
-        g.wait_ge(T.sem.sent, n)
+    wait(GOT3)
+    g.wait_ge(T.sem.sent, plan["sent"][core])
     g.dma_start(out=T.y[:, :], in_=T.land[:, :]).then_inc(T.sem.stored, 16)
     g.wait_ge(T.sem.stored, 16)

import concourse.bass as bass

W = 128
HOLD = 2
SCRATCH = {
    "land": ("sbuf", [128, 4 * W], "float32"),
    "hold": ("sbuf", [128, HOLD * W], "float32"),
}
SEMAPHORES = ["loaded", "near1", "far1", "got2", "got3", "sent", "stored"]

TABLE = """10003 10013 20335 33520;11300 11320 22035;12022 12035 22213 31300;13520 13536 23600 30013
10102 20210 20232 33225;11017 21701 21722 32225 32232;12527 22712 22732 31201 31210;13201 13225 20103 30310
10200 10215 20037 33722;11516 21602 21624 32422 32437;12215 12237 21516 31602;13731 23102 23122 30215
10301 20112 20133 33327 33334;11203 11227 22734;12734 23405 30503 30512;13403 13437 20312 23727
10417 10431 23132 33224;11704 20436 33624 33631;12426 22617 22631 31704;13104 13133 20417 23324
10507 20714 20736 33621;11412 11421 21205 22136;12114 12136 21417 31705;13621 22113 31305 31314
10611 21126 32633;11106 11126 22633;12633 23306 30611;13324 22411 22426 31106
10716 10730 23032 33223;11615 21507 21523 32330;12325 12330 22516 31607;13037 23707 23723 30716"""

NEAR1, FAR1, GOT2, GOT3 = 0, 1, 2, 3
CACHE = {}


def build(T, topo):
    groups = T.tables["GROUPS"]
    table = [[[tuple(int(ch) for ch in tok) for tok in blk.split()] for blk in line.split(";")]
             for line in TABLE.split("\n")]
    writes = []
    for j, grp in enumerate(groups):
        chip = [c - c % 8 for c in grp]
        for s in range(4):
            route = table[j % 8][s]
            senders = set((a, i) for lev, a, i, b, k in route)
            came = {}
            for lev, a, i, b, k in sorted(route):
                src, dst = chip[a] + i, chip[b] + k
                if not topo.may_write(src, dst):
                    raise ValueError("core %d may not write to core %d" % (src, dst))
                if (src != grp[s]) if lev == 1 else (src not in came):
                    raise ValueError("core %d does not hold the block it sends" % src)
                crosses = topo.rack(a) != topo.rack(b)
                writes.append([lev, src, grp[s], dst, crosses, came.get(src, False), (b, k) not in senders])
                came[dst] = crosses
            if any(c != grp[s] and c not in came for c in grp):
                raise ValueError("a member is left without a block")

    stages = {}
    for w in writes:
        stage = 0 if w[0] == 1 else (3 if w[0] == 3 else (2 if w[5] else 1))
        stages.setdefault(w[1], {}).setdefault(stage, []).append(w)
    for per in stages.values():
        if 1 in per and 2 in per and 3 in per and all(w[6] for w in per[2]):
            per[3] = per[3] + per.pop(2)
        if 1 in per and 2 in per and all(w[6] and not w[4] for w in per[1]):
            per[2] = per[2] + per.pop(1)

    where = {}
    for grp in groups:
        for c in grp:
            for k, b in enumerate(grp):
                where[(c, b)] = ("land", k)
    held = {}
    for w in writes:
        if (w[3], w[2]) not in where:
            n = held.get(w[3], 0)
            if n >= HOLD:
                raise ValueError("core %d holds too many blocks" % w[3])
            held[w[3]] = n + 1
            where[(w[3], w[2])] = ("hold", n)

    calls, due, sent = {}, {}, {}
    for src, per in stages.items():
        for stage, ws in per.items():
            transfers = {}
            for w in ws:
                if stage == 0:
                    sem = FAR1 if (w[4] and 1 in stages.get(w[3], {})) else NEAR1
                else:
                    sem = GOT2 if stage < 3 else GOT3
                transfers.setdefault((w[2], sem), []).append(w[3])
            n = 8
            while n * len(transfers) > 8:
                n //= 2
            items = []
            for q, key in enumerate(sorted(transfers)):
                items.append((key[0], key[1], transfers[key], ((1 << n) - 1) << (q * n)))
                sent[src] = sent.get(src, 0) + n
                for d in transfers[key]:
                    due[(d, key[1])] = due.get((d, key[1]), 0) + n
            calls[(src, stage)] = items
    return {"where": where, "calls": calls, "due": due, "sent": sent}


def rank_program(g, core, T, topo):
    if "plan" not in CACHE:
        CACHE["plan"] = build(T, topo)
    plan = CACHE["plan"]
    bufs = {"land": T.land, "hold": T.hold}
    sems = [T.sem.near1, T.sem.far1, T.sem.got2, T.sem.got3]

    def at(c, blk):
        name, k = plan["where"][(c, blk)]
        return bufs[name][:, k * W:(k + 1) * W]

    def call(stage):
        items = plan["calls"].get((core, stage))
        if not items:
            return
        transfers = []
        for blk, sem, dsts, mask in items:
            ids = []
            for d in dsts:
                rid, pid = topo.addr(d, core)
                ids.append(bass.DstId(rid=rid, pnc=pid))
            transfers.append(bass.RemoteDMATransfer(dst_ids=ids, dma_engine_mask=mask, remote_sem=sems[sem],
                                                    srcs=[at(core, blk)], dsts=[at(d, blk) for d in dsts]))
        g.remote_dma_fused(transfers, local_sem=T.sem.sent)

    def wait(sem):
        n = plan["due"].get((core, sem), 0)
        if n:
            g.wait_ge(sems[sem], n)

    g.dma_start(out=at(core, core), in_=T.x[:, :]).then_inc(T.sem.loaded, 16)
    g.wait_ge(T.sem.loaded, 16)
    call(0)
    wait(NEAR1)
    call(1)
    wait(FAR1)
    call(2)
    wait(GOT2)
    call(3)
    wait(GOT3)
    g.wait_ge(T.sem.sent, plan["sent"][core])
    g.dma_start(out=T.y[:, :], in_=T.land[:, :]).then_inc(T.sem.stored, 16)
    g.wait_ge(T.sem.stored, 16)
